import numpy as np
import ml_dtypes


def mxq(x, axis, fmt="e4m3"):
    dtype, down = {"e4m3": (ml_dtypes.float8_e4m3fn, 7), "e5m2": (ml_dtypes.float8_e5m2, 14)}[fmt]
    v = np.moveaxis(np.asarray(x, np.float32).astype(ml_dtypes.bfloat16).astype(np.float64), axis, -1)
    blocks = v.reshape(v.shape[:-1] + (-1, 32))
    amax = np.abs(blocks).max(-1, keepdims=True)
    byte = np.maximum(np.where(amax > 0, np.frexp(amax)[1] - 1 + 127, 0) - down, 1)
    scale = np.exp2(byte - 127.0)
    codes = (blocks / scale).astype(np.float32).astype(dtype).astype(np.float64)
    return np.moveaxis((codes * scale).reshape(v.shape), -1, axis)


WIDE = False


def mx_kscale(k):
    if not WIDE:
        return np.ones(k)
    levels = np.array([30, -30])
    if k % 512:
        return np.exp2(np.random.permutation(np.resize(levels, k // 32))).repeat(32)
    a = np.empty((k // 512, 16))
    for p in range(k // 512):
        a[p, :8] = np.random.permutation(np.resize(levels, 8))
        for g in range(8):
            far = levels[np.abs(levels - a[p, g]) >= 10]
            a[p, g + 8] = far[np.random.randint(len(far))]
    return np.exp2(a.ravel()).repeat(32)


def f64(x):
    return np.asarray(x).astype(np.float64)


def striped(idx):
    return np.tile(np.asarray(idx).reshape(-1, 16).T, (8, 1)).astype(np.uint16)


def unstriped(offs):
    return offs[:16].T.reshape(-1).astype(np.int64)


E2M1 = np.array([0.0, 0.5, 1.0, 1.5, 2.0, 3.0, 4.0, 6.0, -0.0, -0.5, -1.0, -1.5, -2.0, -3.0, -4.0, -6.0])


def pack_weight(w, fmt):
    k, n = w.shape
    w = f64(np.asarray(w, np.float32).astype(ml_dtypes.bfloat16)).reshape(k // 32, 32, n)
    amax = np.abs(w).max(1)
    if fmt in ("e4m3", "e5m2"):
        byte = np.frexp(amax)[1] - 1 + 127 - (7 if fmt == "e4m3" else 14)
    else:
        mant, ex = np.frexp(amax / 6.0)
        byte = np.where(mant > 0.5, ex, ex - 1) + 127
    byte = np.clip(np.where(amax > 0, byte, 1), 1, 254)
    scaled = (w * np.exp2(127.0 - byte)[:, None, :]).reshape(k, n).astype(np.float32)
    by_word = np.ascontiguousarray(scaled.reshape(k // 512, 128, 4, n).transpose(0, 1, 3, 2))
    if fmt in ("e4m3", "e5m2"):
        words = by_word.astype(ml_dtypes.float8_e4m3fn if fmt == "e4m3" else ml_dtypes.float8_e5m2).view(np.uint8)
    else:
        c = by_word.astype(ml_dtypes.float4_e2m1fn).view(np.uint8) & 0xF
        words = (c[..., 0::2] | (c[..., 1::2] << 4)).reshape(k // 512, 128, 2 * n)
    return np.ascontiguousarray(words), np.ascontiguousarray(byte.astype(np.uint8).reshape(k // 512, 16, n))


def unpack_weight(words, scales, fmt):
    g, _, n = scales.shape
    words = np.ascontiguousarray(words).reshape(g, 128, n, -1)
    if fmt in ("e4m3", "e5m2"):
        vals = words.view(ml_dtypes.float8_e4m3fn if fmt == "e4m3" else ml_dtypes.float8_e5m2).astype(np.float64)
    else:
        nib = np.empty((g, 128, n, 4), np.uint8)
        nib[..., 0::2] = words & 0xF
        nib[..., 1::2] = words >> 4
        vals = E2M1[nib]
    vals = vals * np.repeat(np.exp2(scales.astype(np.float64) - 127.0), 8, axis=1)[..., None]
    return vals.transpose(0, 1, 3, 2).reshape(g * 512, n)


K, T, Z, J, R, C, N, L, E = 512, 1024, 1024, 256, 512, 512, 256, 512, 1024


def setup_inputs():
    n = np.random.standard_normal
    idx = np.random.permutation(T)[:J]
    idx2 = np.random.permutation(Z)[:J]
    idx3 = np.random.permutation(C)[:J]
    idx4 = np.random.permutation(C)[:J]
    idx5 = np.random.permutation(E)[:J]
    fk = mx_kscale(K)
    fr = mx_kscale(R)
    fl = mx_kscale(L)
    xtp = pack_weight(n((K, T)) / fk[:, None], "e5m2")
    xop = pack_weight(n((K, Z)) / fk[:, None], "e4m3")
    wp = pack_weight(n((K, R)) * 1 / np.sqrt(K) * fk[:, None] * fr, "e2m1")
    wbp = pack_weight(n((R, N)) * 1 / np.sqrt(R) / fr[:, None], "e2m1")
    sxp = pack_weight(n((L, J)) / fl[:, None], "e4m3")
    wsp = pack_weight(n((L, N)) * 1 / np.sqrt(L) * fl[:, None], "e2m1")
    return {
        "xt_words": xtp[0],
        "xt_scales": xtp[1],
        "xo_words": xop[0],
        "xo_scales": xop[1],
        "w_words": wp[0],
        "w_scales": wp[1],
        "wb_words": wbp[0],
        "wb_scales": wbp[1],
        "sx_words": sxp[0],
        "sx_scales": sxp[1],
        "ws_words": wsp[0],
        "ws_scales": wsp[1],
        "offs": striped(idx),
        "offs2": striped(idx2),
        "offs3": striped(idx3),
        "offs4": striped(idx4),
        "offs5": striped(idx5),
    }


def reference(xt_words, xt_scales, xo_words, xo_scales, w_words, w_scales, wb_words, wb_scales, sx_words, sx_scales, ws_words, ws_scales, offs, offs2, offs3, offs4, offs5):
    idx = unstriped(offs)
    idx2 = unstriped(offs2)
    idx3 = unstriped(offs3)
    idx4 = unstriped(offs4)
    idx5 = unstriped(offs5)
    xtu = unpack_weight(xt_words, xt_scales, "e5m2")
    xou = unpack_weight(xo_words, xo_scales, "e4m3")
    wu = unpack_weight(w_words, w_scales, "e2m1")
    wbu = unpack_weight(wb_words, wb_scales, "e2m1")
    sxu = unpack_weight(sx_words, sx_scales, "e4m3")
    wsu = unpack_weight(ws_words, ws_scales, "e2m1")
    xtidxg = xtu[:, idx]
    a = wu.T @ xtidxg
    xoidx2g = xou[:, idx2]
    b = wu.T @ xoidx2g
    pw = np.zeros((R, C))
    pw[:, idx3] = a
    hid = np.maximum(pw[:, idx4], b)
    hidq = mxq(hid, 0, "e4m3")
    p = wbu.T @ hidq + wsu.T @ sxu
    y = np.zeros((N, E))
    y[:, idx5] = p
    return y

@@ -1,0 +1,187 @@
+from contextlib import ExitStack
+
+import concourse.mybir as mybir
+
+F32 = mybir.dt.float32
+BF16 = mybir.dt.bfloat16
+I32 = mybir.dt.int32
+U32 = mybir.dt.uint32
+U16 = mybir.dt.uint16
+U8 = mybir.dt.uint8
+E4M3 = mybir.dt.float8_e4m3fn_x4
+E5M2 = mybir.dt.float8_e5m2_x4
+E2M1 = mybir.dt.float4_e2m1fn_x4
+COPY = mybir.ActivationFunctionType.Copy
+MAX = mybir.AluOpType.max
+
+P = 128
+PACK = 4
+T, Z, J, R, C, N, E = 1024, 1024, 256, 512, 512, 256, 1024
+HALF = J // 2
+LIST_COLS = J // 16
+HALF_COLS = LIST_COLS // 2
+
+FLOPS = 2 * 512 * R * J * 2 + 2 * R * N * J + 2 * 512 * N * J
+
+
+def tile_list_oneforboth_board_skip_scattered_kernel(
+    tc, xt_words, xt_scales, xo_words, xo_scales, w_words, w_scales, wb_words, wb_scales,
+    sx_words, sx_scales, ws_words, ws_scales, offs, offs2, offs3, offs4, offs5, out,
+):
+    nc = tc.nc
+
+    with ExitStack() as ctx:
+        sb = ctx.enter_context(tc.tile_pool(name="sb", bufs=1))
+        ps = ctx.enter_context(tc.psum_pool(name="ps", bufs=1))
+
+        def tile(name, shape, dtype, tag=None):
+            return sb.tile(shape, dtype, name=name, tag=tag or name, align_bytes=64)
+
+        def load_list(name, src):
+            t = sb.tile([P, LIST_COLS], U16, name=name)
+            nc.sync.dma_start(t[:], src)
+            return t
+
+        def load_fp8_words(name, src, width, queue=nc.sync):
+            t = tile(name, [P, width], U32)
+            queue.dma_start(t[:].bitcast(I32), src[0].rearrange("p c r -> p (c r)").bitcast(I32))
+            return t
+
+        def load_fp4_words(name, src, width, queue=nc.sync):
+            t = tile(name, [P, 2 * width], U8)
+            queue.dma_start(t[:].bitcast(I32), src[0].bitcast(I32))
+            return t
+
+        def zeroed_plane(name, width):
+            t = tile(name, [P, width], U8)
+            nc.vector.memset(t[:].bitcast(I32), 0)
+            return t
+
+        def load_scale_rows(plane, src, queue=nc.sync, quadrants=range(4)):
+            for q in quadrants:
+                queue.dma_start(plane[32 * q : 32 * q + 4, :].bitcast(I32), src[0, 4 * q : 4 * q + 4, :].bitcast(I32))
+
+        xt_s = zeroed_plane("xt_s", T)
+        w_s_raw = zeroed_plane("w_s_raw", R)
+        xo_s = zeroed_plane("xo_s", Z)
+        late_s = zeroed_plane("late_s", J + 2 * N)
+        sx_s, ws_s, wb_s = late_s[:, 0:J], late_s[:, J : J + N], late_s[:, J + N : J + 2 * N]
+        board = [tile(f"board{t}", [P, C], F32) for t in range(PACK)]
+        for t in (0, 2, 1, 3):
+            nc.vector.memset(board[t][:], 0.0)
+
+        idx = load_list("idx", offs)
+        w_raw = load_fp4_words("w_raw", w_words, R)
+        load_scale_rows(xt_s, xt_scales)
+        xt_w = load_fp8_words("xt_w", xt_words, T)
+        load_scale_rows(w_s_raw, w_scales)
+        xo_w = load_fp8_words("xo_w", xo_words, Z)
+        idx2 = load_list("idx2", offs2)
+        load_scale_rows(xo_s, xo_scales)
+        idx3 = load_list("idx3", offs3)
+        idx4 = load_list("idx4", offs4)
+        sx_w = load_fp8_words("sx_w", sx_words, J)
+        ws_w = load_fp4_words("ws_w", ws_words, N)
+        load_scale_rows(sx_s, sx_scales)
+        load_scale_rows(ws_s, ws_scales)
+        wb_w = load_fp4_words("wb_w", wb_words, N)
+        load_scale_rows(wb_s, wb_scales)
+        idx5 = load_list("idx5", offs5)
+
+        w_w = tile("w_w", [P, 2 * R], U8)
+        nc.vector.tensor_copy(
+            w_w[:].bitcast(U16).rearrange("p (t q) -> p t q", t=PACK),
+            w_raw[:].bitcast(U16).rearrange("p (q t) -> p t q", t=PACK),
+        )
+        xtg_s = tile("xtg_s", [P, J], U8)
+        nc.vector.tensor_copy(xtg_s[:], xt_s[:].indirect(idx[:]))
+        xtg_w = tile("xtg_w", [P, J], U32)
+        nc.vector.tensor_copy(xtg_w[:], xt_w[:].indirect(idx[:]))
+        w_s = [tile(f"w_s{t}", [P, P], U8) for t in range(PACK)]
+
+        def w_slice(t):
+            return dict(lhsT=w_w[:, 2 * P * t : 2 * P * (t + 1)].bitcast(E2M1), lhsT_scale=w_s[t][:])
+
+        a_ps = {}
+        for t in (0, 2, 1, 3):
+            nc.vector.tensor_copy(w_s[t][:], w_s_raw[:].rearrange("p (q t) -> p t q", t=PACK)[:, t, :])
+            a_ps[t] = ps.tile([P, J], F32, name=f"a_ps{t}", tag=f"bank{t}")
+            nc.tensor.matmul_mx(a_ps[t][:], rhs=xtg_w[:].bitcast(E5M2), rhs_scale=xtg_s[:], start=True, stop=True, **w_slice(t))
+
+        def s_move(dst, src):
+            nc.scalar.activation(dst, src, COPY)
+
+        def v_move(dst, src):
+            nc.vector.tensor_copy(dst, src)
+
+        a_sb = [tile(f"a_sb{t}", [P, J], F32) for t in range(PACK)]
+        for t in (0, 2, 1, 3):
+            s_move(a_sb[t][:], a_ps[t][:])
+
+        def place_a(move, t):
+            move(board[t][:].indirect(idx3[:]), a_sb[t][:])
+
+        xog_w = tile("xog_w", [P, J], U32)
+        nc.vector.tensor_copy(xog_w[:], xo_w[:].indirect(idx2[:]))
+        place_a(v_move, 0)
+        place_a(s_move, 2)
+        xog_s = tile("xog_s", [P, J], U8)
+        nc.vector.tensor_copy(xog_s[:], xo_s[:].indirect(idx2[:]))
+        place_a(v_move, 1)
+        place_a(s_move, 3)
+
+        page = [tile("page0", [P, E], F32, tag="xo_w"), tile("page1", [P, E], F32, tag="xo_s")]
+        for n in range(2):
+            nc.gpsimd.memset(page[n][:], 0.0)
+
+        b_ps = []
+        for h in range(2):
+            bank = ps.tile([P, PACK, HALF], F32, name=f"b_ps{h}")
+            cols = slice(HALF * h, HALF * (h + 1))
+            for t in range(PACK):
+                nc.tensor.matmul_mx(bank[:, t, :], rhs=xog_w[:, cols].bitcast(E4M3), rhs_scale=xog_s[:, cols], start=True, stop=True, **w_slice(t))
+            b_ps.append(bank)
+
+        p_ps = {}
+        for h in range(2):
+            cols = slice(HALF * h, HALF * (h + 1))
+            for n in range(2):
+                p_ps[n, h] = ps.tile([P, HALF], F32, name=f"p_ps{n}{h}", tag=f"bank{2 * h + n}")
+                nc.tensor.matmul_mx(
+                    p_ps[n, h][:],
+                    lhsT=ws_w[:, 2 * P * n : 2 * P * (n + 1)].bitcast(E2M1), lhsT_scale=ws_s[:, P * n : P * (n + 1)],
+                    rhs=sx_w[:, cols].bitcast(E4M3), rhs_scale=sx_s[:, cols], start=True, stop=False,
+                )
+
+        picked = [tile(f"picked{h}", [P, PACK, HALF], F32) for h in range(2)]
+
+        def pick(move, t, h):
+            move(picked[h][:, t, :], board[t][:].indirect(idx4[:, HALF_COLS * h : HALF_COLS * (h + 1)]))
+
+        for t in range(PACK):
+            pick(v_move if t < 2 else s_move, t, 0)
+        for t in range(PACK):
+            pick(v_move if t < 1 else s_move, t, 1)
+
+        for h in range(2):
+            hid = tile(f"hid{h}", [P, HALF, PACK], BF16, tag="hid")
+            nc.vector.tensor_tensor(hid[:], picked[h][:].rearrange("p t j -> p j t"), b_ps[h][:].rearrange("p t j -> p j t"), MAX)
+            hid_w = tile(f"hid_w{h}", [P, HALF], U32)
+            hid_s = tile(f"hid_s{h}", [P, HALF], U8)
+            nc.vector.quantize_mx(hid_w[:].bitcast(E4M3), hid_s[:], hid[:].rearrange("p j t -> p (j t)"))
+            for n in range(2):
+                nc.tensor.matmul_mx(
+                    p_ps[n, h][:],
+                    lhsT=wb_w[:, 2 * P * n : 2 * P * (n + 1)].bitcast(E2M1), lhsT_scale=wb_s[:, P * n : P * (n + 1)],
+                    rhs=hid_w[:].bitcast(E4M3), rhs_scale=hid_s[:], start=False, stop=True,
+                )
+
+        for h in range(2):
+            p_sb = [tile(f"p_sb{n}{h}", [P, HALF], F32) for n in range(2)]
+            for n in range(2):
+                s_move(p_sb[n][:], p_ps[n, h][:])
+            for n, move in ((0, s_move), (1, v_move)):
+                move(page[n][:].indirect(idx5[:, HALF_COLS * h : HALF_COLS * (h + 1)]), p_sb[n][:])
+
+        for n in range(2):
+            nc.sync.dma_start(out[P * n : P * (n + 1), :], page[n][:])

@@ -79,14 +79,15 @@ def tile_list_oneforboth_board_skip_scattered_kernel(
         idx2 = load_list("idx2", offs2)
         load_scale_rows(xo_s, xo_scales)
         idx3 = load_list("idx3", offs3)
-        idx4 = load_list("idx4", offs4)
+        for plane, src in ((sx_s, sx_scales), (ws_s, ws_scales), (wb_s, wb_scales)):
+            nc.sync.dma_start(plane[0:16, :].bitcast(I32), src[0].bitcast(I32))
         sx_w = load_fp8_words("sx_w", sx_words, J)
         ws_w = load_fp4_words("ws_w", ws_words, N)
-        load_scale_rows(sx_s, sx_scales)
-        load_scale_rows(ws_s, ws_scales)
         wb_w = load_fp4_words("wb_w", wb_words, N)
-        load_scale_rows(wb_s, wb_scales)
         idx5 = load_list("idx5", offs5)
+        for q in range(1, 4):
+            nc.sync.dma_start(late_s[32 * q : 32 * q + 4, :].bitcast(I32), late_s[4 * q : 4 * q + 4, :].bitcast(I32))
+        idx4 = load_list("idx4", offs4)
 
         w_w = tile("w_w", [P, 2 * R], U8)
         nc.vector.tensor_copy(
@@ -176,12 +177,12 @@ def tile_list_oneforboth_board_skip_scattered_kernel(
                     rhs=hid_w[:].bitcast(E4M3), rhs_scale=hid_s[:], start=False, stop=True,
                 )
 
-        for h in range(2):
+        for h, copy_out, placers in ((0, s_move, (s_move, s_move)), (1, v_move, (v_move, s_move))):
             p_sb = [tile(f"p_sb{n}{h}", [P, HALF], F32) for n in range(2)]
             for n in range(2):
-                s_move(p_sb[n][:], p_ps[n, h][:])
-            for n, move in ((0, s_move), (1, v_move)):
-                move(page[n][:].indirect(idx5[:, HALF_COLS * h : HALF_COLS * (h + 1)]), p_sb[n][:])
+                copy_out(p_sb[n][:], p_ps[n, h][:])
+            for n in range(2):
+                placers[n](page[n][:].indirect(idx5[:, HALF_COLS * h : HALF_COLS * (h + 1)]), p_sb[n][:])
 
         for n in range(2):
             nc.sync.dma_start(out[P * n : P * (n + 1), :], page[n][:])

@@ -85,9 +85,9 @@ def tile_list_oneforboth_board_skip_scattered_kernel(
         ws_w = load_fp4_words("ws_w", ws_words, N)
         wb_w = load_fp4_words("wb_w", wb_words, N)
         idx5 = load_list("idx5", offs5)
+        idx4 = load_list("idx4", offs4)
         for q in range(1, 4):
             nc.sync.dma_start(late_s[32 * q : 32 * q + 4, :].bitcast(I32), late_s[4 * q : 4 * q + 4, :].bitcast(I32))
-        idx4 = load_list("idx4", offs4)
 
         w_w = tile("w_w", [P, 2 * R], U8)
         nc.vector.tensor_copy(
@@ -165,8 +165,13 @@ def tile_list_oneforboth_board_skip_scattered_kernel(
             pick(v_move if t < 1 else s_move, t, 1)
 
         for h in range(2):
-            hid = tile(f"hid{h}", [P, HALF, PACK], BF16, tag="hid")
-            nc.vector.tensor_tensor(hid[:], picked[h][:].rearrange("p t j -> p j t"), b_ps[h][:].rearrange("p t j -> p j t"), MAX)
+            hid = tile(f"hid{h}", [P, HALF, PACK], BF16, tag=("hid0", "sx_w")[h])
+            nc.vector.tensor_tensor(
+                hid[:].rearrange("p (c i) t -> p c t i", i=4),
+                picked[h][:].rearrange("p t (c i) -> p c t i", i=4),
+                b_ps[h][:].rearrange("p t (c i) -> p c t i", i=4),
+                MAX,
+            )
             hid_w = tile(f"hid_w{h}", [P, HALF], U32)
             hid_s = tile(f"hid_s{h}", [P, HALF], U8)
             nc.vector.quantize_mx(hid_w[:].bitcast(E4M3), hid_s[:], hid[:].rearrange("p j t -> p (j t)"))
@@ -177,7 +182,7 @@ def tile_list_oneforboth_board_skip_scattered_kernel(
                     rhs=hid_w[:].bitcast(E4M3), rhs_scale=hid_s[:], start=False, stop=True,
                 )
 
-        for h, copy_out, placers in ((0, s_move, (s_move, s_move)), (1, v_move, (v_move, s_move))):
+        for h, copy_out, placers in ((0, s_move, (s_move, s_move)), (1, v_move, (v_move, v_move))):
             p_sb = [tile(f"p_sb{n}{h}", [P, HALF], F32) for n in range(2)]
             for n in range(2):
                 copy_out(p_sb[n][:], p_ps[n, h][:])

@@ -69,6 +69,9 @@ def tile_list_oneforboth_board_skip_scattered_kernel(
         board = [tile(f"board{t}", [P, C], F32) for t in range(PACK)]
         for t in (0, 2, 1, 3):
             nc.vector.memset(board[t][:], 0.0)
+        page = [tile(f"page{n}", [P, E], F32) for n in range(2)]
+        for n in range(2):
+            nc.vector.memset(page[n][:], 0.0)
 
         idx = load_list("idx", offs)
         w_raw = load_fp4_words("w_raw", w_words, R)
@@ -130,10 +133,6 @@ def tile_list_oneforboth_board_skip_scattered_kernel(
         nc.vector.tensor_copy(xog_s[:], xo_s[:].indirect(idx2[:]))
         place_a(v_move, 1)
         place_a(s_move, 3)
-
-        page = [tile("page0", [P, E], F32, tag="xo_w"), tile("page1", [P, E], F32, tag="xo_s")]
-        for n in range(2):
-            nc.gpsimd.memset(page[n][:], 0.0)
 
         b_ps = []
         for h in range(2):

from contextlib import ExitStack

import concourse.mybir as mybir

F32 = mybir.dt.float32
BF16 = mybir.dt.bfloat16
I32 = mybir.dt.int32
U32 = mybir.dt.uint32
U16 = mybir.dt.uint16
U8 = mybir.dt.uint8
E4M3 = mybir.dt.float8_e4m3fn_x4
E5M2 = mybir.dt.float8_e5m2_x4
E2M1 = mybir.dt.float4_e2m1fn_x4
COPY = mybir.ActivationFunctionType.Copy
MAX = mybir.AluOpType.max

P = 128
PACK = 4
T, Z, J, R, C, N, E = 1024, 1024, 256, 512, 512, 256, 1024
HALF = J // 2
LIST_COLS = J // 16
HALF_COLS = LIST_COLS // 2

FLOPS = 2 * 512 * R * J * 2 + 2 * R * N * J + 2 * 512 * N * J


def tile_list_oneforboth_board_skip_scattered_kernel(
    tc, xt_words, xt_scales, xo_words, xo_scales, w_words, w_scales, wb_words, wb_scales,
    sx_words, sx_scales, ws_words, ws_scales, offs, offs2, offs3, offs4, offs5, out,
):
    nc = tc.nc

    with ExitStack() as ctx:
        sb = ctx.enter_context(tc.tile_pool(name="sb", bufs=1))
        ps = ctx.enter_context(tc.psum_pool(name="ps", bufs=1))

        def tile(name, shape, dtype, tag=None):
            return sb.tile(shape, dtype, name=name, tag=tag or name, align_bytes=64)

        def load_list(name, src):
            t = sb.tile([P, LIST_COLS], U16, name=name)
            nc.sync.dma_start(t[:], src)
            return t

        def load_fp8_words(name, src, width, queue=nc.sync):
            t = tile(name, [P, width], U32)
            queue.dma_start(t[:].bitcast(I32), src[0].rearrange("p c r -> p (c r)").bitcast(I32))
            return t

        def load_fp4_words(name, src, width, queue=nc.sync):
            t = tile(name, [P, 2 * width], U8)
            queue.dma_start(t[:].bitcast(I32), src[0].bitcast(I32))
            return t

        def zeroed_plane(name, width):
            t = tile(name, [P, width], U8)
            nc.vector.memset(t[:].bitcast(I32), 0)
            return t

        def load_scale_rows(plane, src, queue=nc.sync, quadrants=range(4)):
            for q in quadrants:
                queue.dma_start(plane[32 * q : 32 * q + 4, :].bitcast(I32), src[0, 4 * q : 4 * q + 4, :].bitcast(I32))

        xt_s = zeroed_plane("xt_s", T)
        w_s_raw = zeroed_plane("w_s_raw", R)
        xo_s = zeroed_plane("xo_s", Z)
        late_s = zeroed_plane("late_s", J + 2 * N)
        sx_s, ws_s, wb_s = late_s[:, 0:J], late_s[:, J : J + N], late_s[:, J + N : J + 2 * N]
        board = [tile(f"board{t}", [P, C], F32) for t in range(PACK)]
        for t in (0, 2, 1, 3):
            nc.vector.memset(board[t][:], 0.0)
        page = [tile(f"page{n}", [P, E], F32) for n in range(2)]
        for n in range(2):
            nc.vector.memset(page[n][:], 0.0)

        idx = load_list("idx", offs)
        w_raw = load_fp4_words("w_raw", w_words, R)
        load_scale_rows(xt_s, xt_scales)
        xt_w = load_fp8_words("xt_w", xt_words, T)
        load_scale_rows(w_s_raw, w_scales)
        xo_w = load_fp8_words("xo_w", xo_words, Z)
        idx2 = load_list("idx2", offs2)
        load_scale_rows(xo_s, xo_scales)
        idx3 = load_list("idx3", offs3)
        for plane, src in ((sx_s, sx_scales), (ws_s, ws_scales), (wb_s, wb_scales)):
            nc.sync.dma_start(plane[0:16, :].bitcast(I32), src[0].bitcast(I32))
        sx_w = load_fp8_words("sx_w", sx_words, J)
        ws_w = load_fp4_words("ws_w", ws_words, N)
        wb_w = load_fp4_words("wb_w", wb_words, N)
        idx5 = load_list("idx5", offs5)
        idx4 = load_list("idx4", offs4)
        for q in range(1, 4):
            nc.sync.dma_start(late_s[32 * q : 32 * q + 4, :].bitcast(I32), late_s[4 * q : 4 * q + 4, :].bitcast(I32))

        w_w = tile("w_w", [P, 2 * R], U8)
        nc.vector.tensor_copy(
            w_w[:].bitcast(U16).rearrange("p (t q) -> p t q", t=PACK),
            w_raw[:].bitcast(U16).rearrange("p (q t) -> p t q", t=PACK),
        )
        xtg_s = tile("xtg_s", [P, J], U8)
        nc.vector.tensor_copy(xtg_s[:], xt_s[:].indirect(idx[:]))
        xtg_w = tile("xtg_w", [P, J], U32)
        nc.vector.tensor_copy(xtg_w[:], xt_w[:].indirect(idx[:]))
        w_s = [tile(f"w_s{t}", [P, P], U8) for t in range(PACK)]

        def w_slice(t):
            return dict(lhsT=w_w[:, 2 * P * t : 2 * P * (t + 1)].bitcast(E2M1), lhsT_scale=w_s[t][:])

        a_ps = {}
        for t in (0, 2, 1, 3):
            nc.vector.tensor_copy(w_s[t][:], w_s_raw[:].rearrange("p (q t) -> p t q", t=PACK)[:, t, :])
            a_ps[t] = ps.tile([P, J], F32, name=f"a_ps{t}", tag=f"bank{t}")
            nc.tensor.matmul_mx(a_ps[t][:], rhs=xtg_w[:].bitcast(E5M2), rhs_scale=xtg_s[:], start=True, stop=True, **w_slice(t))

        def s_move(dst, src):
            nc.scalar.activation(dst, src, COPY)

        def v_move(dst, src):
            nc.vector.tensor_copy(dst, src)

        a_sb = [tile(f"a_sb{t}", [P, J], F32) for t in range(PACK)]
        for t in (0, 2, 1, 3):
            s_move(a_sb[t][:], a_ps[t][:])

        def place_a(move, t):
            move(board[t][:].indirect(idx3[:]), a_sb[t][:])

        xog_w = tile("xog_w", [P, J], U32)
        nc.vector.tensor_copy(xog_w[:], xo_w[:].indirect(idx2[:]))
        place_a(v_move, 0)
        place_a(s_move, 2)
        xog_s = tile("xog_s", [P, J], U8)
        nc.vector.tensor_copy(xog_s[:], xo_s[:].indirect(idx2[:]))
        place_a(v_move, 1)
        place_a(s_move, 3)

        b_ps = []
        for h in range(2):
            bank = ps.tile([P, PACK, HALF], F32, name=f"b_ps{h}")
            cols = slice(HALF * h, HALF * (h + 1))
            for t in range(PACK):
                nc.tensor.matmul_mx(bank[:, t, :], rhs=xog_w[:, cols].bitcast(E4M3), rhs_scale=xog_s[:, cols], start=True, stop=True, **w_slice(t))
            b_ps.append(bank)

        p_ps = {}
        for h in range(2):
            cols = slice(HALF * h, HALF * (h + 1))
            for n in range(2):
                p_ps[n, h] = ps.tile([P, HALF], F32, name=f"p_ps{n}{h}", tag=f"bank{2 * h + n}")
                nc.tensor.matmul_mx(
                    p_ps[n, h][:],
                    lhsT=ws_w[:, 2 * P * n : 2 * P * (n + 1)].bitcast(E2M1), lhsT_scale=ws_s[:, P * n : P * (n + 1)],
                    rhs=sx_w[:, cols].bitcast(E4M3), rhs_scale=sx_s[:, cols], start=True, stop=False,
                )

        picked = [tile(f"picked{h}", [P, PACK, HALF], F32) for h in range(2)]

        def pick(move, t, h):
            move(picked[h][:, t, :], board[t][:].indirect(idx4[:, HALF_COLS * h : HALF_COLS * (h + 1)]))

        for t in range(PACK):
            pick(v_move if t < 2 else s_move, t, 0)
        for t in range(PACK):
            pick(v_move if t < 1 else s_move, t, 1)

        for h in range(2):
            hid = tile(f"hid{h}", [P, HALF, PACK], BF16, tag=("hid0", "sx_w")[h])
            nc.vector.tensor_tensor(
                hid[:].rearrange("p (c i) t -> p c t i", i=4),
                picked[h][:].rearrange("p t (c i) -> p c t i", i=4),
                b_ps[h][:].rearrange("p t (c i) -> p c t i", i=4),
                MAX,
            )
            hid_w = tile(f"hid_w{h}", [P, HALF], U32)
            hid_s = tile(f"hid_s{h}", [P, HALF], U8)
            nc.vector.quantize_mx(hid_w[:].bitcast(E4M3), hid_s[:], hid[:].rearrange("p j t -> p (j t)"))
            for n in range(2):
                nc.tensor.matmul_mx(
                    p_ps[n, h][:],
                    lhsT=wb_w[:, 2 * P * n : 2 * P * (n + 1)].bitcast(E2M1), lhsT_scale=wb_s[:, P * n : P * (n + 1)],
                    rhs=hid_w[:].bitcast(E4M3), rhs_scale=hid_s[:], start=False, stop=True,
                )

        for h, copy_out, placers in ((0, s_move, (s_move, s_move)), (1, v_move, (v_move, v_move))):
            p_sb = [tile(f"p_sb{n}{h}", [P, HALF], F32) for n in range(2)]
            for n in range(2):
                copy_out(p_sb[n][:], p_ps[n, h][:])
            for n in range(2):
                placers[n](page[n][:].indirect(idx5[:, HALF_COLS * h : HALF_COLS * (h + 1)]), p_sb[n][:])

        for n in range(2):
            nc.sync.dma_start(out[P * n : P * (n + 1), :], page[n][:])
